import numpy as np
import ml_dtypes


def mxq(x, axis, fmt="e4m3"):
    dtype, down = {"e4m3": (ml_dtypes.float8_e4m3fn, 7), "e5m2": (ml_dtypes.float8_e5m2, 14)}[fmt]
    v = np.moveaxis(np.asarray(x, np.float32).astype(ml_dtypes.bfloat16).astype(np.float64), axis, -1)
    blocks = v.reshape(v.shape[:-1] + (-1, 32))
    amax = np.abs(blocks).max(-1, keepdims=True)
    byte = np.maximum(np.where(amax > 0, np.frexp(amax)[1] - 1 + 127, 0) - down, 1)
    scale = np.exp2(byte - 127.0)
    codes = (blocks / scale).astype(np.float32).astype(dtype).astype(np.float64)
    return np.moveaxis((codes * scale).reshape(v.shape), -1, axis)


WIDE = False


def mx_kscale(k):
    if not WIDE:
        return np.ones(k)
    levels = np.array([24, -24, 12, -12, 0])
    if k % 512:
        return np.exp2(np.random.permutation(np.resize(levels, k // 32))).repeat(32)
    a = np.empty((k // 512, 16))
    for p in range(k // 512):
        a[p, :8] = np.random.permutation(np.resize(levels, 8))
        for g in range(8):
            far = levels[np.abs(levels - a[p, g]) >= 10]
            a[p, g + 8] = far[np.random.randint(len(far))]
    return np.exp2(a.ravel()).repeat(32)


def f64(x):
    return np.asarray(x).astype(np.float64)


def striped8(idx):
    return np.concatenate([v.reshape(-1, 16).T for v in idx]).astype(np.uint16)


def unstriped8(offs):
    return np.stack([offs[16 * g:16 * g + 16].T.reshape(-1) for g in range(8)]).astype(np.int64)


def planes(y):
    n, m = y.shape
    v = y.astype(np.float32).astype(ml_dtypes.bfloat16).astype(np.float64).reshape(n // 32, 32, m)
    top = np.abs(v).max(1)
    byte = np.clip(np.where(top > 0, np.frexp(top)[1] - 1 + 127 - 7, 1), 1, 254)
    codes = (v * np.exp2(127.0 - byte)[:, None, :]).reshape(n, m).astype(np.float32).astype(ml_dtypes.float8_e4m3fn).view(np.uint8)
    words = codes.reshape(n // 512, 128, 4, m).transpose(0, 1, 3, 2)
    return np.ascontiguousarray(words), np.ascontiguousarray(byte.astype(np.uint8).reshape(n // 512, 16, m))


K, L, N, T, J = 1024, 512, 512, 2048, 1024


def setup_inputs():
    n = np.random.standard_normal
    s = mx_kscale(K)[:, None]
    s2 = mx_kscale(L)[:, None]
    return {
        "xT": (n((K, T)) * s).astype(np.float32),
        "wgt": np.repeat(np.random.uniform(0.5, 2.0, (8, J)), 16, axis=0).astype(np.float32),
        "wt": (n((K, N)) / np.sqrt(K) / s).astype(np.float32),
        "c": (n((L, J)) * s2).astype(np.float32),
        "wx": (n((L, N)) / np.sqrt(L) / s2).astype(np.float32),
        "b": (0.3 * n(N)).astype(np.float32),
        "offs": striped8(np.stack([np.random.permutation(T)[:J] for _ in range(8)])),
    }


def reference(xT, wgt, wt, c, wx, b, offs):
    idx = unstriped8(offs)
    rows = np.arange(K)
    xg = f64(wgt)[rows // 4 % 128] * f64(xT)[rows[:, None], idx[rows % 512 // 64]]
    xT_ = mxq(xg, 0, "e4m3")
    wt_q_ = mxq(f64(wt), 0, "e4m3")
    wt_r_ = mxq(f64(wt) - wt_q_, 0, "e4m3")
    c_ = mxq(f64(c), 0, "e4m3")
    wx_ = mxq(f64(wx), 0, "e4m3")
    y = wt_q_.T @ xT_ + wt_r_.T @ xT_ + wx_.T @ c_
    out_0 = y + f64(b)[:, None]
    return (out_0,) + planes(out_0)

@@ -1,0 +1,225 @@
+from contextlib import ExitStack
+
+import concourse.mybir as mybir
+from concourse.masks import make_identity
+
+K, L, N, T, J = 1024, 512, 512, 2048, 1024
+FLOPS = 2 * (2 * K * N * J + L * N * J + 512 * K * N)
+
+F32 = mybir.dt.float32
+BF16 = mybir.dt.bfloat16
+I32 = mybir.dt.int32
+U32 = mybir.dt.uint32
+U16 = mybir.dt.uint16
+U8 = mybir.dt.uint8
+FP8X4 = mybir.dt.float8_e4m3fn_x4
+ALU = mybir.AluOpType
+ACT = mybir.ActivationFunctionType
+
+P = 128
+PACK = 4
+KP = P * PACK
+HALF = J // 2
+CHUNK = J // 4
+LIST_ROWS = 16
+MH = 64
+
+
+def tile_list_tier_biasP_kernel(tc, xT, wgt, wt, c, wx, b, offs, out_0, out_1, out_2):
+    nc = tc.nc
+    with ExitStack() as ctx:
+        keep = ctx.enter_context(tc.tile_pool(name="keep", bufs=1))
+        ring = ctx.enter_context(tc.tile_pool(name="ring", bufs=2))
+        psum = ctx.enter_context(tc.psum_pool(name="psum", bufs=1))
+
+        offsets = keep.tile([P, J // LIST_ROWS], U16, name="offsets")
+        x_sb = [keep.tile([P, T], F32, name=f"x{r}") for r in range(2 * PACK)]
+        wgt_sb = [keep.tile([P, HALF], F32, name=f"wgt{h}") for h in range(2)]
+        wt_sb = [keep.tile([P, PACK, N], F32, name=f"wt{a}") for a in range(2)]
+        wx_sb = keep.tile([P, PACK, N], F32, name="wx_sb")
+        c_sb = [keep.tile([P, PACK, HALF], F32, name=f"c{h}") for h in range(2)]
+        b_sb = keep.tile([P, PACK], F32, name="b_sb")
+
+        x_planes = xT.rearrange("(a p i) t -> a i p t", a=2, i=PACK)
+        wt_rows = wt.rearrange("(a p i) n -> a p i n", a=2, i=PACK)
+        c_rows = c.rearrange("(p i) j -> p i j", i=PACK)
+
+        def load_x(r):
+            nc.sync.dma_start(out=x_sb[r][:], in_=x_planes[r // PACK, r % PACK])
+
+        def load_wgt(h):
+            nc.sync.dma_start(out=wgt_sb[h][:], in_=wgt[:, h * HALF:(h + 1) * HALF])
+
+        def load_wt(a):
+            nc.sync.dma_start(out=wt_sb[a][:], in_=wt_rows[a])
+
+        def load_c(h):
+            nc.sync.dma_start(out=c_sb[h][:], in_=c_rows[:, :, h * HALF:(h + 1) * HALF])
+
+        nc.sync.dma_start(offsets[:], offs)
+        load_wgt(0)
+        load_x(0)
+        load_wt(0)
+        load_wgt(1)
+        load_x(1)
+        load_wt(1)
+        load_x(2)
+        load_x(3)
+        nc.sync.dma_start(out=wx_sb[:], in_=wx.rearrange("(p i) n -> p i n", i=PACK))
+        load_x(4)
+        load_x(5)
+        load_c(0)
+        load_x(6)
+        load_x(7)
+        nc.sync.dma_start(out=b_sb[:], in_=b.rearrange("(p t) -> p t", t=PACK))
+        load_c(1)
+
+        def mx_tiles(name, width):
+            codes = keep.tile([P, width], U32, name=name + "_codes", align_bytes=64)
+            scales = keep.tile([P, width], U8, name=name + "_scales", align_bytes=64)
+            return codes, scales
+
+        def quantize(mx, cols, grouped):
+            nc.vector.quantize_mx(out=mx[0][:, cols].bitcast(FP8X4), scales=mx[1][:, cols], in_=grouped)
+
+        def matmul(out, lhs, lhs_cols, rhs, rhs_cols, start, stop):
+            nc.tensor.matmul_mx(
+                out=out,
+                lhsT=lhs[0][:, lhs_cols].bitcast(FP8X4), lhsT_scale=lhs[1][:, lhs_cols],
+                rhs=rhs[0][:, rhs_cols].bitcast(FP8X4), rhs_scale=rhs[1][:, rhs_cols],
+                start=start, stop=stop,
+            )
+
+        def staging(width):
+            return ring.tile([P, PACK * width], BF16, name=f"staged{width}", tag=f"staged{width}", bufs=6, align_bytes=64)
+
+        eye = keep.tile([P, P], BF16, name="eye")
+        make_identity(nc, eye[:])
+        eye_grouped = staging(KP)
+        nc.vector.memset(eye_grouped[:], 0.0)
+        eye_view = eye_grouped[:].rearrange("p (s m i) -> p s m i", s=PACK, i=PACK)
+        for i in range(PACK):
+            nc.vector.tensor_copy(out=eye_view[:, i, :, i], in_=eye[:])
+        eye_mx = mx_tiles("eye", KP)
+        quantize(eye_mx, slice(0, KP), eye_grouped[:])
+
+        def round_weights(raw):
+            grouped = staging(N)
+            nc.scalar.activation(
+                out=grouped[:].rearrange("p (t m i) -> p m i t", t=PACK, i=PACK),
+                in_=raw[:].rearrange("p i (m t) -> p m i t", t=PACK),
+                func=ACT.Identity,
+            )
+            return grouped
+
+        def round_columns(copy, raw, width):
+            grouped = staging(width)
+            copy(
+                out=grouped[:].rearrange("p (u v i) -> p u i v", v=PACK, i=PACK),
+                in_=raw.rearrange("p i (u v) -> p u i v", v=PACK),
+            )
+            return grouped
+
+        def gather(r, dst, j0, width):
+            h, o = divmod(j0, HALF)
+            nc.vector.tensor_tensor(
+                dst, x_sb[r][:].indirect(offsets[:, j0 // LIST_ROWS:(j0 + width) // LIST_ROWS]),
+                wgt_sb[h][:, o:o + width], ALU.mult,
+            )
+
+        wq_mx = [mx_tiles(f"wq{a}", N) for a in range(2)]
+        wr_mx = [mx_tiles(f"wr{a}", N) for a in range(2)]
+        wx_mx = mx_tiles("wx", N)
+        xg0_mx = [mx_tiles(f"xg0{h}", HALF) for h in range(2)]
+        xg1_mx = [mx_tiles(f"xg1{q}", CHUNK) for q in range(4)]
+        c_mx = [mx_tiles(f"cq{h}", HALF) for h in range(2)]
+        y_mx = mx_tiles("y", J)
+
+        def bank(n):
+            return psum.tile([P, 512], F32, name=f"bank{n}", tag=f"bank{n}")
+
+        def first_tier(a):
+            quantize(wq_mx[a], slice(0, N), round_weights(wt_sb[a])[:])
+
+        def second_tier(a):
+            grouped = staging(N)
+            dealt = grouped[:].rearrange("p (t m i) -> p t m i", t=PACK, i=PACK)
+            raw = wt_sb[a][:].rearrange("p i (m t) -> p i m t", t=PACK)
+            for s in range(4):
+                t0, m0 = 2 * (s // 2), MH * (s % 2)
+                back = bank(4 + s)[:].rearrange("p (i t m) -> p i t m", i=PACK, t=2)
+                for i in range(PACK):
+                    for t in range(2):
+                        col = (t0 + t) * P + m0
+                        matmul(back[:, i, t, :], eye_mx, slice(i * P, (i + 1) * P), wq_mx[a], slice(col, col + MH), True, True)
+                nc.vector.tensor_tensor(
+                    dealt[:, t0:t0 + 2, m0:m0 + MH, :].rearrange("p t m i -> p m i t"),
+                    raw[:, :, m0:m0 + MH, t0:t0 + 2].rearrange("p i m t -> p m i t"),
+                    back.rearrange("p i t m -> p m i t"),
+                    ALU.subtract,
+                )
+            quantize(wr_mx[a], slice(0, N), grouped[:])
+
+        picked0 = [ring.tile([P, PACK, HALF], F32, name=f"picked0{h}", tag="wide") for h in range(2)]
+
+        def gather_pass0(r):
+            for h in range(2):
+                gather(r, picked0[h][:, r, :], h * HALF, HALF)
+
+        gather_pass0(0)
+        first_tier(0)
+        gather_pass0(1)
+        second_tier(0)
+        first_tier(1)
+        gather_pass0(2)
+        second_tier(1)
+        gather_pass0(3)
+        for h in range(2):
+            quantize(xg0_mx[h], slice(0, HALF), round_columns(nc.scalar.copy, picked0[h][:], HALF)[:])
+        quantize(wx_mx, slice(0, N), round_weights(wx_sb)[:])
+        quantize(c_mx[0], slice(0, HALF), round_columns(nc.scalar.copy, c_sb[0][:], HALF)[:])
+
+        out_rows = out_0.rearrange("(p t) j -> p t j", t=PACK)
+        words = out_1[0].rearrange("p j i -> p (j i)").bitcast(I32)
+        all_cols = slice(0, CHUNK)
+
+        def front(q):
+            picked = ring.tile([P, PACK, CHUNK], F32, name="picked1", tag="picked1")
+            for i in range(PACK):
+                gather(PACK + i, picked[:, i, :], q * CHUNK, CHUNK)
+            quantize(xg1_mx[q], all_cols, round_columns(nc.scalar.copy, picked[:], CHUNK)[:])
+
+        def back_end(q):
+            h, o = divmod(q * CHUNK, HALF)
+            half_cols = slice(o, o + CHUNK)
+            y = ring.tile([P, PACK, CHUNK], F32, name="y", tag="y", bufs=4)
+            for u in range(2):
+                acc = bank(2 * q + u)[:].rearrange("p (t j) -> p t j", t=2)
+                terms = [(wq_mx[0], xg0_mx[h], half_cols), (wr_mx[0], xg0_mx[h], half_cols), (wx_mx, c_mx[h], half_cols),
+                         (wq_mx[1], xg1_mx[q], all_cols), (wr_mx[1], xg1_mx[q], all_cols)]
+                for n, (lhs, rhs, cols) in enumerate(terms):
+                    for t in range(2):
+                        w_cols = slice((2 * u + t) * P, (2 * u + t + 1) * P)
+                        matmul(acc[:, t, :], lhs, w_cols, rhs, cols, n == 0 and t == 0, n == len(terms) - 1 and t == 1)
+                for t in range(2):
+                    row = 2 * u + t
+                    nc.scalar.activation(out=y[:, row, :], in_=acc[:, t, :], func=ACT.Identity, bias=b_sb[:, row:row + 1])
+            j_cols = slice(q * CHUNK, (q + 1) * CHUNK)
+            nc.sync.dma_start(out=out_rows[:, :, j_cols], in_=y[:])
+            quantize(y_mx, j_cols, round_columns(nc.vector.tensor_copy, y[:], CHUNK)[:])
+            nc.sync.dma_start(out=words[:, j_cols], in_=y_mx[0][:, j_cols].bitcast(I32))
+
+        front(0)
+        front(1)
+        back_end(0)
+        quantize(c_mx[1], slice(0, HALF), round_columns(nc.scalar.copy, c_sb[1][:], HALF)[:])
+        front(2)
+        back_end(1)
+        front(3)
+        back_end(2)
+        back_end(3)
+
+        scale_rows = out_2[0].bitcast(I32)
+        for g in range(4):
+            queue = nc.sync if g % 2 == 0 else nc.scalar
+            queue.dma_start(out=scale_rows[4 * g:4 * g + 4, :], in_=y_mx[1][32 * g:32 * g + 4, :].bitcast(I32))

@@ -1,7 +1,6 @@
 from contextlib import ExitStack
 
 import concourse.mybir as mybir
-from concourse.masks import make_identity
 
 K, L, N, T, J = 1024, 512, 512, 2048, 1024
 FLOPS = 2 * (2 * K * N * J + L * N * J + 512 * K * N)
@@ -23,6 +22,8 @@ HALF = J // 2
 CHUNK = J // 4
 LIST_ROWS = 16
 MH = 64
+CHUNKS = [256, 256, 256, 256]
+STARTS = [sum(CHUNKS[:q]) for q in range(len(CHUNKS))]
 
 
 def tile_list_tier_biasP_kernel(tc, xT, wgt, wt, c, wx, b, offs, out_0, out_1, out_2):
@@ -33,7 +34,7 @@ def tile_list_tier_biasP_kernel(tc, xT, wgt, wt, c, wx, b, offs, out_0, out_1, o
         psum = ctx.enter_context(tc.psum_pool(name="psum", bufs=1))
 
         offsets = keep.tile([P, J // LIST_ROWS], U16, name="offsets")
-        x_sb = [keep.tile([P, T], F32, name=f"x{r}") for r in range(2 * PACK)]
+        x_sb = [ring.tile([P, T], F32, name=f"x{r}", tag=f"held{r}", bufs=1, align_bytes=64) for r in range(2 * PACK)]
         wgt_sb = [keep.tile([P, HALF], F32, name=f"wgt{h}") for h in range(2)]
         wt_sb = [keep.tile([P, PACK, N], F32, name=f"wt{a}") for a in range(2)]
         wx_sb = keep.tile([P, PACK, N], F32, name="wx_sb")
@@ -57,25 +58,25 @@ def tile_list_tier_biasP_kernel(tc, xT, wgt, wt, c, wx, b, offs, out_0, out_1, o
             nc.sync.dma_start(out=c_sb[h][:], in_=c_rows[:, :, h * HALF:(h + 1) * HALF])
 
         nc.sync.dma_start(offsets[:], offs)
+        load_wt(0)
         load_wgt(0)
         load_x(0)
-        load_wt(0)
         load_wgt(1)
-        load_x(1)
         load_wt(1)
+        load_x(1)
+        nc.sync.dma_start(out=wx_sb[:], in_=wx.rearrange("(p i) n -> p i n", i=PACK))
         load_x(2)
         load_x(3)
-        nc.sync.dma_start(out=wx_sb[:], in_=wx.rearrange("(p i) n -> p i n", i=PACK))
         load_x(4)
-        load_x(5)
         load_c(0)
+        load_x(5)
+        load_c(1)
         load_x(6)
         load_x(7)
         nc.sync.dma_start(out=b_sb[:], in_=b.rearrange("(p t) -> p t", t=PACK))
-        load_c(1)
 
         def mx_tiles(name, width):
-            codes = keep.tile([P, width], U32, name=name + "_codes", align_bytes=64)
+            codes = ring.tile([P, width], U32, name=name + "_codes", tag="held" + name, bufs=1, align_bytes=64)
             scales = keep.tile([P, width], U8, name=name + "_scales", align_bytes=64)
             return codes, scales
 
@@ -90,35 +91,52 @@ def tile_list_tier_biasP_kernel(tc, xT, wgt, wt, c, wx, b, offs, out_0, out_1, o
                 start=start, stop=stop,
             )
 
-        def staging(width):
-            return ring.tile([P, PACK * width], BF16, name=f"staged{width}", tag=f"staged{width}", bufs=6, align_bytes=64)
+        def staging(width, tag=None):
+            if tag is None:
+                return ring.tile([P, PACK * width], BF16, name=f"staged{width}", tag=f"staged{width}", bufs=5, align_bytes=64)
+            return ring.tile([P, PACK * width], BF16, name="held", tag=tag, bufs=1, align_bytes=64)
 
-        eye = keep.tile([P, P], BF16, name="eye")
-        make_identity(nc, eye[:])
-        eye_grouped = staging(KP)
+        ones = keep.tile([P, P], F32, name="ones")
+        column = keep.tile([P, P], F32, name="column", align_bytes=64)
+        turned = keep.tile([P, P], F32, name="turned", align_bytes=64)
+        eye_grouped = keep.tile([P, PACK * (KP + 1)], BF16, name="eye_grouped", align_bytes=64)
+        nc.vector.memset(ones[:], 1.0)
         nc.vector.memset(eye_grouped[:], 0.0)
-        eye_view = eye_grouped[:].rearrange("p (s m i) -> p s m i", s=PACK, i=PACK)
-        for i in range(PACK):
-            nc.vector.tensor_copy(out=eye_view[:, i, :, i], in_=eye[:])
+        nc.vector.tensor_tensor_scan(column[:], ones[:], ones[:], -1.0, ALU.mult, ALU.add)
+        nc.vector.transpose(turned[:], column[:])
+        diagonal = eye_grouped[:].rearrange("p (s r) -> p s r", s=PACK)
+        for g in range(4):
+            part = slice(32 * g, 32 * g + 32)
+            nc.vector.tensor_tensor(
+                diagonal[part, :, PACK * 32 * g:PACK * 32 * (g + 1):PACK],
+                column[part, part].unsqueeze(1).to_broadcast([32, PACK, 32]),
+                turned[part, part].unsqueeze(1).to_broadcast([32, PACK, 32]),
+                ALU.is_equal,
+            )
         eye_mx = mx_tiles("eye", KP)
-        quantize(eye_mx, slice(0, KP), eye_grouped[:])
+        quantize(eye_mx, slice(0, KP), eye_grouped[:, :PACK * KP])
 
-        def round_weights(raw):
-            grouped = staging(N)
-            nc.scalar.activation(
+        def scalar_copy(out, in_):
+            nc.scalar.activation(out=out, in_=in_, func=ACT.Identity)
+
+        def round_weights(copy, raw, tag=None):
+            grouped = staging(N, tag)
+            copy(
                 out=grouped[:].rearrange("p (t m i) -> p m i t", t=PACK, i=PACK),
                 in_=raw[:].rearrange("p i (m t) -> p m i t", t=PACK),
-                func=ACT.Identity,
             )
             return grouped
 
-        def round_columns(copy, raw, width):
-            grouped = staging(width)
+        def round_columns(copy, raw, width, tag=None):
+            grouped = staging(width, tag)
             copy(
                 out=grouped[:].rearrange("p (u v i) -> p u i v", v=PACK, i=PACK),
                 in_=raw.rearrange("p i (u v) -> p u i v", v=PACK),
             )
             return grouped
+
+        picked0 = [ring.tile([P, PACK, HALF], F32, name=f"picked0{h}", tag="wide") for h in range(2)]
+        picked1 = {}
 
         def gather(r, dst, j0, width):
             h, o = divmod(j0, HALF)
@@ -127,22 +145,30 @@ def tile_list_tier_biasP_kernel(tc, xT, wgt, wt, c, wx, b, offs, out_0, out_1, o
                 wgt_sb[h][:, o:o + width], ALU.mult,
             )
 
+        def gather0(r, h):
+            gather(r, picked0[h][:, r, :], h * HALF, HALF)
+
+        def gather1(r, q, tag="picked1", bufs=2):
+            if q not in picked1:
+                picked1.setdefault(q, ring.tile([P, PACK, CHUNKS[q]], F32, name="picked1", tag=tag, bufs=bufs, align_bytes=64))
+            gather(r, picked1[q][:, r - PACK, :], STARTS[q], CHUNKS[q])
+
         wq_mx = [mx_tiles(f"wq{a}", N) for a in range(2)]
         wr_mx = [mx_tiles(f"wr{a}", N) for a in range(2)]
         wx_mx = mx_tiles("wx", N)
         xg0_mx = [mx_tiles(f"xg0{h}", HALF) for h in range(2)]
-        xg1_mx = [mx_tiles(f"xg1{q}", CHUNK) for q in range(4)]
+        xg1_mx = [mx_tiles(f"xg1{q}", w) for q, w in enumerate(CHUNKS)]
         c_mx = [mx_tiles(f"cq{h}", HALF) for h in range(2)]
         y_mx = mx_tiles("y", J)
 
         def bank(n):
             return psum.tile([P, 512], F32, name=f"bank{n}", tag=f"bank{n}")
 
-        def first_tier(a):
-            quantize(wq_mx[a], slice(0, N), round_weights(wt_sb[a])[:])
+        def first_tier(a, copy, tag=None):
+            quantize(wq_mx[a], slice(0, N), round_weights(copy, wt_sb[a], tag)[:])
 
-        def second_tier(a):
-            grouped = staging(N)
+        def second_tier(a, tag=None):
+            grouped = staging(N, tag)
             dealt = grouped[:].rearrange("p (t m i) -> p t m i", t=PACK, i=PACK)
             raw = wt_sb[a][:].rearrange("p i (m t) -> p i m t", t=PACK)
             for s in range(4):
@@ -160,64 +186,93 @@ def tile_list_tier_biasP_kernel(tc, xT, wgt, wt, c, wx, b, offs, out_0, out_1, o
                 )
             quantize(wr_mx[a], slice(0, N), grouped[:])
 
-        picked0 = [ring.tile([P, PACK, HALF], F32, name=f"picked0{h}", tag="wide") for h in range(2)]
-
-        def gather_pass0(r):
-            for h in range(2):
-                gather(r, picked0[h][:, r, :], h * HALF, HALF)
-
-        gather_pass0(0)
-        first_tier(0)
-        gather_pass0(1)
-        second_tier(0)
-        first_tier(1)
-        gather_pass0(2)
-        second_tier(1)
-        gather_pass0(3)
-        for h in range(2):
-            quantize(xg0_mx[h], slice(0, HALF), round_columns(nc.scalar.copy, picked0[h][:], HALF)[:])
-        quantize(wx_mx, slice(0, N), round_weights(wx_sb)[:])
-        quantize(c_mx[0], slice(0, HALF), round_columns(nc.scalar.copy, c_sb[0][:], HALF)[:])
-
         out_rows = out_0.rearrange("(p t) j -> p t j", t=PACK)
         words = out_1[0].rearrange("p j i -> p (j i)").bitcast(I32)
-        all_cols = slice(0, CHUNK)
+        results = {}
 
-        def front(q):
-            picked = ring.tile([P, PACK, CHUNK], F32, name="picked1", tag="picked1")
-            for i in range(PACK):
-                gather(PACK + i, picked[:, i, :], q * CHUNK, CHUNK)
-            quantize(xg1_mx[q], all_cols, round_columns(nc.scalar.copy, picked[:], CHUNK)[:])
+        def front(q, tag=None, copy=nc.scalar.copy):
+            quantize(xg1_mx[q], slice(0, CHUNKS[q]), round_columns(copy, picked1[q][:], CHUNKS[q], tag)[:])
 
-        def back_end(q):
-            h, o = divmod(q * CHUNK, HALF)
-            half_cols = slice(o, o + CHUNK)
-            y = ring.tile([P, PACK, CHUNK], F32, name="y", tag="y", bufs=4)
-            for u in range(2):
-                acc = bank(2 * q + u)[:].rearrange("p (t j) -> p t j", t=2)
-                terms = [(wq_mx[0], xg0_mx[h], half_cols), (wr_mx[0], xg0_mx[h], half_cols), (wx_mx, c_mx[h], half_cols),
-                         (wq_mx[1], xg1_mx[q], all_cols), (wr_mx[1], xg1_mx[q], all_cols)]
+        def features(quarter, copy, tag=None):
+            h, o = divmod(quarter * CHUNK, HALF)
+            quantize(c_mx[h], slice(o, o + CHUNK), round_columns(copy, c_sb[h][:, :, o:o + CHUNK], CHUNK, tag)[:])
+
+        def product(q, on_vector):
+            width = CHUNKS[q]
+            h, o = divmod(STARTS[q], HALF)
+            half_cols = slice(o, o + width)
+            own_cols = slice(0, width)
+            per_bank = 512 // width
+            y = keep.tile([P, PACK, width], F32, name=f"y{q}")
+            results.setdefault(q, y)
+            terms = [(wq_mx[0], xg0_mx[h], half_cols), (wr_mx[0], xg0_mx[h], half_cols), (wx_mx, c_mx[h], half_cols),
+                     (wq_mx[1], xg1_mx[q], own_cols), (wr_mx[1], xg1_mx[q], own_cols)]
+            for t0 in range(0, PACK, per_bank):
+                acc = bank((STARTS[q] * PACK + t0 * width) // 512)[:].rearrange("p (t j) -> p t j", t=per_bank)
                 for n, (lhs, rhs, cols) in enumerate(terms):
-                    for t in range(2):
-                        w_cols = slice((2 * u + t) * P, (2 * u + t + 1) * P)
-                        matmul(acc[:, t, :], lhs, w_cols, rhs, cols, n == 0 and t == 0, n == len(terms) - 1 and t == 1)
-                for t in range(2):
-                    row = 2 * u + t
-                    nc.scalar.activation(out=y[:, row, :], in_=acc[:, t, :], func=ACT.Identity, bias=b_sb[:, row:row + 1])
-            j_cols = slice(q * CHUNK, (q + 1) * CHUNK)
-            nc.sync.dma_start(out=out_rows[:, :, j_cols], in_=y[:])
-            quantize(y_mx, j_cols, round_columns(nc.vector.tensor_copy, y[:], CHUNK)[:])
+                    for t in range(per_bank):
+                        w_cols = slice((t0 + t) * P, (t0 + t + 1) * P)
+                        matmul(acc[:, t, :], lhs, w_cols, rhs, cols, n == 0 and t == 0,
+                               n == len(terms) - 1 and t == per_bank - 1)
+                if on_vector and t0 + per_bank == PACK:
+                    bias = b_sb[:, t0:t0 + per_bank].unsqueeze(2).to_broadcast([P, per_bank, width])
+                    nc.vector.tensor_tensor(y[:, t0:t0 + per_bank, :], acc, bias, ALU.add)
+                else:
+                    for t in range(per_bank):
+                        row = t0 + t
+                        nc.scalar.activation(out=y[:, row, :], in_=acc[:, t, :], func=ACT.Identity, bias=b_sb[:, row:row + 1])
+                nc.sync.dma_start(out=out_rows[:, t0:t0 + per_bank, STARTS[q]:STARTS[q] + width], in_=y[:, t0:t0 + per_bank, :])
+
+        def planes(q, copy, tag=None):
+            j_cols = slice(STARTS[q], STARTS[q] + CHUNKS[q])
+            quantize(y_mx, j_cols, round_columns(copy, results[q][:], CHUNKS[q], tag)[:])
             nc.sync.dma_start(out=words[:, j_cols], in_=y_mx[0][:, j_cols].bitcast(I32))
 
+        first_tier(0, nc.vector.tensor_copy)
+        gather0(0, 0)
+        gather0(0, 1)
+        second_tier(0, "held0")
+        first_tier(1, scalar_copy)
+        gather0(1, 0)
+        gather0(1, 1)
+        quantize(wx_mx, slice(0, N), round_weights(scalar_copy, wx_sb)[:])
+        gather0(2, 0)
+        gather0(2, 1)
+        gather0(3, 0)
+        gather0(3, 1)
+        second_tier(1, "held3")
+        quantize(xg0_mx[0], slice(0, HALF), round_columns(nc.scalar.copy, picked0[0][:], HALF)[:])
+        quantize(xg0_mx[1], slice(0, HALF), round_columns(nc.scalar.copy, picked0[1][:], HALF)[:])
+        gather1(4, 0)
+        gather1(4, 1)
+        quantize(c_mx[0], slice(0, HALF), round_columns(nc.scalar.copy, c_sb[0][:], HALF)[:])
+        gather1(5, 0)
+        gather1(5, 1)
+        quantize(c_mx[1], slice(0, HALF), round_columns(nc.scalar.copy, c_sb[1][:], HALF)[:])
+        gather1(6, 0)
+        gather1(6, 1)
+        gather1(7, 0)
+        gather1(7, 1)
         front(0)
         front(1)
-        back_end(0)
-        quantize(c_mx[1], slice(0, HALF), round_columns(nc.scalar.copy, c_sb[1][:], HALF)[:])
+        product(0, False)
+        gather1(4, 2)
+        gather1(5, 2)
+        gather1(6, 2)
+        gather1(7, 2)
         front(2)
-        back_end(1)
+        product(1, False)
+        gather1(4, 3)
+        gather1(5, 3)
+        gather1(6, 3)
+        gather1(7, 3)
         front(3)
-        back_end(2)
-        back_end(3)
+        planes(0, nc.vector.tensor_copy)
+        planes(1, nc.vector.tensor_copy)
+        product(2, False)
+        planes(2, nc.vector.tensor_copy)
+        product(3, False)
+        planes(3, nc.vector.tensor_copy)
 
         scale_rows = out_2[0].bitcast(I32)
         for g in range(4):

@@ -22,7 +22,8 @@ HALF = J // 2
 CHUNK = J // 4
 LIST_ROWS = 16
 MH = 64
-CHUNKS = [256, 256, 256, 256]
+CHUNKS = [256, 256, 256, 128, 128]
+CODE_STORES = {1: 0, 3: 512, 4: 896}
 STARTS = [sum(CHUNKS[:q]) for q in range(len(CHUNKS))]
 
 
@@ -57,15 +58,15 @@ def tile_list_tier_biasP_kernel(tc, xT, wgt, wt, c, wx, b, offs, out_0, out_1, o
         def load_c(h):
             nc.sync.dma_start(out=c_sb[h][:], in_=c_rows[:, :, h * HALF:(h + 1) * HALF])
 
-        nc.sync.dma_start(offsets[:], offs)
         load_wt(0)
+        nc.sync.dma_start(offsets[:], offs)
         load_wgt(0)
         load_x(0)
         load_wgt(1)
         load_wt(1)
         load_x(1)
-        nc.sync.dma_start(out=wx_sb[:], in_=wx.rearrange("(p i) n -> p i n", i=PACK))
         load_x(2)
+        nc.sync.dma_start(out=wx_sb[:], in_=wx.rearrange("(p i) n -> p i n", i=PACK))
         load_x(3)
         load_x(4)
         load_c(0)
@@ -97,22 +98,21 @@ def tile_list_tier_biasP_kernel(tc, xT, wgt, wt, c, wx, b, offs, out_0, out_1, o
             return ring.tile([P, PACK * width], BF16, name="held", tag=tag, bufs=1, align_bytes=64)
 
         ones = keep.tile([P, P], F32, name="ones")
+        shift = keep.tile([P, 1], F32, name="shift")
         column = keep.tile([P, P], F32, name="column", align_bytes=64)
-        turned = keep.tile([P, P], F32, name="turned", align_bytes=64)
+        turned = keep.tile([P, 32], F32, name="turned", align_bytes=64)
         eye_grouped = keep.tile([P, PACK * (KP + 1)], BF16, name="eye_grouped", align_bytes=64)
-        nc.vector.memset(ones[:], 1.0)
-        nc.vector.memset(eye_grouped[:], 0.0)
-        nc.vector.tensor_tensor_scan(column[:], ones[:], ones[:], -1.0, ALU.mult, ALU.add)
-        nc.vector.transpose(turned[:], column[:])
-        diagonal = eye_grouped[:].rearrange("p (s r) -> p s r", s=PACK)
         for g in range(4):
-            part = slice(32 * g, 32 * g + 32)
-            nc.vector.tensor_tensor(
-                diagonal[part, :, PACK * 32 * g:PACK * 32 * (g + 1):PACK],
-                column[part, part].unsqueeze(1).to_broadcast([32, PACK, 32]),
-                turned[part, part].unsqueeze(1).to_broadcast([32, PACK, 32]),
-                ALU.is_equal,
-            )
+            nc.gpsimd.memset(shift[32 * g:32 * g + 32, :], -32.0 * g)
+        nc.gpsimd.memset(eye_grouped[:].bitcast(I32), 0)
+        nc.vector.memset(ones[:], 1.0)
+        nc.vector.tensor_tensor_scan(column[:], ones[:], ones[:], shift[:], ALU.mult, ALU.add)
+        nc.vector.transpose(turned[:], column[:, :32])
+        nc.vector.tensor_scalar(
+            eye_grouped[:].rearrange("p (s r) -> p s r", s=PACK)[:, :, 0:KP:PACK],
+            column[:].unsqueeze(1).to_broadcast([P, PACK, P]),
+            shift[:], turned[:, 0:1], ALU.add, ALU.is_equal,
+        )
         eye_mx = mx_tiles("eye", KP)
         quantize(eye_mx, slice(0, KP), eye_grouped[:, :PACK * KP])
 
@@ -125,6 +125,14 @@ def tile_list_tier_biasP_kernel(tc, xT, wgt, wt, c, wx, b, offs, out_0, out_1, o
                 out=grouped[:].rearrange("p (t m i) -> p m i t", t=PACK, i=PACK),
                 in_=raw[:].rearrange("p i (m t) -> p m i t", t=PACK),
             )
+            return grouped
+
+        def round_weights_shared(raw):
+            grouped = staging(N)
+            dst = grouped[:].rearrange("p (t m i) -> p m i t", t=PACK, i=PACK)
+            src = raw[:].rearrange("p i (m t) -> p m i t", t=PACK)
+            nc.vector.tensor_copy(out=dst[:, :MH], in_=src[:, :MH])
+            scalar_copy(out=dst[:, MH:], in_=src[:, MH:])
             return grouped
 
         def round_columns(copy, raw, width, tag=None):
@@ -148,7 +156,7 @@ def tile_list_tier_biasP_kernel(tc, xT, wgt, wt, c, wx, b, offs, out_0, out_1, o
         def gather0(r, h):
             gather(r, picked0[h][:, r, :], h * HALF, HALF)
 
-        def gather1(r, q, tag="picked1", bufs=2):
+        def gather1(r, q, tag="picked1", bufs=3):
             if q not in picked1:
                 picked1.setdefault(q, ring.tile([P, PACK, CHUNKS[q]], F32, name="picked1", tag=tag, bufs=bufs, align_bytes=64))
             gather(r, picked1[q][:, r - PACK, :], STARTS[q], CHUNKS[q])
@@ -214,7 +222,7 @@ def tile_list_tier_biasP_kernel(tc, xT, wgt, wt, c, wx, b, offs, out_0, out_1, o
                         w_cols = slice((t0 + t) * P, (t0 + t + 1) * P)
                         matmul(acc[:, t, :], lhs, w_cols, rhs, cols, n == 0 and t == 0,
                                n == len(terms) - 1 and t == per_bank - 1)
-                if on_vector and t0 + per_bank == PACK:
+                if t0 // per_bank in on_vector:
                     bias = b_sb[:, t0:t0 + per_bank].unsqueeze(2).to_broadcast([P, per_bank, width])
                     nc.vector.tensor_tensor(y[:, t0:t0 + per_bank, :], acc, bias, ALU.add)
                 else:
@@ -226,18 +234,20 @@ def tile_list_tier_biasP_kernel(tc, xT, wgt, wt, c, wx, b, offs, out_0, out_1, o
         def planes(q, copy, tag=None):
             j_cols = slice(STARTS[q], STARTS[q] + CHUNKS[q])
             quantize(y_mx, j_cols, round_columns(copy, results[q][:], CHUNKS[q], tag)[:])
-            nc.sync.dma_start(out=words[:, j_cols], in_=y_mx[0][:, j_cols].bitcast(I32))
+            if q in CODE_STORES:
+                done = slice(CODE_STORES[q], STARTS[q] + CHUNKS[q])
+                nc.sync.dma_start(out=words[:, done], in_=y_mx[0][:, done].bitcast(I32))
 
-        first_tier(0, nc.vector.tensor_copy)
+        quantize(wq_mx[0], slice(0, N), round_weights_shared(wt_sb[0])[:])
         gather0(0, 0)
         gather0(0, 1)
         second_tier(0, "held0")
         first_tier(1, scalar_copy)
         gather0(1, 0)
         gather0(1, 1)
-        quantize(wx_mx, slice(0, N), round_weights(scalar_copy, wx_sb)[:])
         gather0(2, 0)
         gather0(2, 1)
+        quantize(wx_mx, slice(0, N), round_weights(scalar_copy, wx_sb)[:])
         gather0(3, 0)
         gather0(3, 1)
         second_tier(1, "held3")
@@ -245,34 +255,41 @@ def tile_list_tier_biasP_kernel(tc, xT, wgt, wt, c, wx, b, offs, out_0, out_1, o
         quantize(xg0_mx[1], slice(0, HALF), round_columns(nc.scalar.copy, picked0[1][:], HALF)[:])
         gather1(4, 0)
         gather1(4, 1)
+        gather1(4, 2)
         quantize(c_mx[0], slice(0, HALF), round_columns(nc.scalar.copy, c_sb[0][:], HALF)[:])
         gather1(5, 0)
         gather1(5, 1)
+        gather1(5, 2)
         quantize(c_mx[1], slice(0, HALF), round_columns(nc.scalar.copy, c_sb[1][:], HALF)[:])
         gather1(6, 0)
         gather1(6, 1)
+        gather1(6, 2)
         gather1(7, 0)
         gather1(7, 1)
+        gather1(7, 2)
         front(0)
         front(1)
-        product(0, False)
-        gather1(4, 2)
-        gather1(5, 2)
-        gather1(6, 2)
-        gather1(7, 2)
-        front(2)
-        product(1, False)
+        product(0, ())
         gather1(4, 3)
         gather1(5, 3)
         gather1(6, 3)
         gather1(7, 3)
+        front(2)
+        product(1, (0, 1))
         front(3)
-        planes(0, nc.vector.tensor_copy)
-        planes(1, nc.vector.tensor_copy)
-        product(2, False)
-        planes(2, nc.vector.tensor_copy)
-        product(3, False)
-        planes(3, nc.vector.tensor_copy)
+        gather1(4, 4)
+        gather1(5, 4)
+        gather1(6, 4)
+        gather1(7, 4)
+        front(4)
+        product(2, (0, 1))
+        product(3, (0,))
+        product(4, (0,))
+        planes(0, nc.scalar.copy)
+        planes(1, nc.scalar.copy)
+        planes(2, nc.scalar.copy)
+        planes(3, nc.scalar.copy)
+        planes(4, nc.vector.tensor_copy)
 
         scale_rows = out_2[0].bitcast(I32)
         for g in range(4):

from contextlib import ExitStack

import concourse.mybir as mybir

K, L, N, T, J = 1024, 512, 512, 2048, 1024
FLOPS = 2 * (2 * K * N * J + L * N * J + 512 * K * N)

F32 = mybir.dt.float32
BF16 = mybir.dt.bfloat16
I32 = mybir.dt.int32
U32 = mybir.dt.uint32
U16 = mybir.dt.uint16
U8 = mybir.dt.uint8
FP8X4 = mybir.dt.float8_e4m3fn_x4
ALU = mybir.AluOpType
ACT = mybir.ActivationFunctionType

P = 128
PACK = 4
KP = P * PACK
HALF = J // 2
CHUNK = J // 4
LIST_ROWS = 16
MH = 64
CHUNKS = [256, 256, 256, 128, 128]
CODE_STORES = {1: 0, 3: 512, 4: 896}
STARTS = [sum(CHUNKS[:q]) for q in range(len(CHUNKS))]


def tile_list_tier_biasP_kernel(tc, xT, wgt, wt, c, wx, b, offs, out_0, out_1, out_2):
    nc = tc.nc
    with ExitStack() as ctx:
        keep = ctx.enter_context(tc.tile_pool(name="keep", bufs=1))
        ring = ctx.enter_context(tc.tile_pool(name="ring", bufs=2))
        psum = ctx.enter_context(tc.psum_pool(name="psum", bufs=1))

        offsets = keep.tile([P, J // LIST_ROWS], U16, name="offsets")
        x_sb = [ring.tile([P, T], F32, name=f"x{r}", tag=f"held{r}", bufs=1, align_bytes=64) for r in range(2 * PACK)]
        wgt_sb = [keep.tile([P, HALF], F32, name=f"wgt{h}") for h in range(2)]
        wt_sb = [keep.tile([P, PACK, N], F32, name=f"wt{a}") for a in range(2)]
        wx_sb = keep.tile([P, PACK, N], F32, name="wx_sb")
        c_sb = [keep.tile([P, PACK, HALF], F32, name=f"c{h}") for h in range(2)]
        b_sb = keep.tile([P, PACK], F32, name="b_sb")

        x_planes = xT.rearrange("(a p i) t -> a i p t", a=2, i=PACK)
        wt_rows = wt.rearrange("(a p i) n -> a p i n", a=2, i=PACK)
        c_rows = c.rearrange("(p i) j -> p i j", i=PACK)

        def load_x(r):
            nc.sync.dma_start(out=x_sb[r][:], in_=x_planes[r // PACK, r % PACK])

        def load_wgt(h):
            nc.sync.dma_start(out=wgt_sb[h][:], in_=wgt[:, h * HALF:(h + 1) * HALF])

        def load_wt(a):
            nc.sync.dma_start(out=wt_sb[a][:], in_=wt_rows[a])

        def load_c(h):
            nc.sync.dma_start(out=c_sb[h][:], in_=c_rows[:, :, h * HALF:(h + 1) * HALF])

        load_wt(0)
        nc.sync.dma_start(offsets[:], offs)
        load_wgt(0)
        load_x(0)
        load_wgt(1)
        load_wt(1)
        load_x(1)
        load_x(2)
        nc.sync.dma_start(out=wx_sb[:], in_=wx.rearrange("(p i) n -> p i n", i=PACK))
        load_x(3)
        load_x(4)
        load_c(0)
        load_x(5)
        load_c(1)
        load_x(6)
        load_x(7)
        nc.sync.dma_start(out=b_sb[:], in_=b.rearrange("(p t) -> p t", t=PACK))

        def mx_tiles(name, width):
            codes = ring.tile([P, width], U32, name=name + "_codes", tag="held" + name, bufs=1, align_bytes=64)
            scales = keep.tile([P, width], U8, name=name + "_scales", align_bytes=64)
            return codes, scales

        def quantize(mx, cols, grouped):
            nc.vector.quantize_mx(out=mx[0][:, cols].bitcast(FP8X4), scales=mx[1][:, cols], in_=grouped)

        def matmul(out, lhs, lhs_cols, rhs, rhs_cols, start, stop):
            nc.tensor.matmul_mx(
                out=out,
                lhsT=lhs[0][:, lhs_cols].bitcast(FP8X4), lhsT_scale=lhs[1][:, lhs_cols],
                rhs=rhs[0][:, rhs_cols].bitcast(FP8X4), rhs_scale=rhs[1][:, rhs_cols],
                start=start, stop=stop,
            )

        def staging(width, tag=None):
            if tag is None:
                return ring.tile([P, PACK * width], BF16, name=f"staged{width}", tag=f"staged{width}", bufs=5, align_bytes=64)
            return ring.tile([P, PACK * width], BF16, name="held", tag=tag, bufs=1, align_bytes=64)

        ones = keep.tile([P, P], F32, name="ones")
        shift = keep.tile([P, 1], F32, name="shift")
        column = keep.tile([P, P], F32, name="column", align_bytes=64)
        turned = keep.tile([P, 32], F32, name="turned", align_bytes=64)
        eye_grouped = keep.tile([P, PACK * (KP + 1)], BF16, name="eye_grouped", align_bytes=64)
        for g in range(4):
            nc.gpsimd.memset(shift[32 * g:32 * g + 32, :], -32.0 * g)
        nc.gpsimd.memset(eye_grouped[:].bitcast(I32), 0)
        nc.vector.memset(ones[:], 1.0)
        nc.vector.tensor_tensor_scan(column[:], ones[:], ones[:], shift[:], ALU.mult, ALU.add)
        nc.vector.transpose(turned[:], column[:, :32])
        nc.vector.tensor_scalar(
            eye_grouped[:].rearrange("p (s r) -> p s r", s=PACK)[:, :, 0:KP:PACK],
            column[:].unsqueeze(1).to_broadcast([P, PACK, P]),
            shift[:], turned[:, 0:1], ALU.add, ALU.is_equal,
        )
        eye_mx = mx_tiles("eye", KP)
        quantize(eye_mx, slice(0, KP), eye_grouped[:, :PACK * KP])

        def scalar_copy(out, in_):
            nc.scalar.activation(out=out, in_=in_, func=ACT.Identity)

        def round_weights(copy, raw, tag=None):
            grouped = staging(N, tag)
            copy(
                out=grouped[:].rearrange("p (t m i) -> p m i t", t=PACK, i=PACK),
                in_=raw[:].rearrange("p i (m t) -> p m i t", t=PACK),
            )
            return grouped

        def round_weights_shared(raw):
            grouped = staging(N)
            dst = grouped[:].rearrange("p (t m i) -> p m i t", t=PACK, i=PACK)
            src = raw[:].rearrange("p i (m t) -> p m i t", t=PACK)
            nc.vector.tensor_copy(out=dst[:, :MH], in_=src[:, :MH])
            scalar_copy(out=dst[:, MH:], in_=src[:, MH:])
            return grouped

        def round_columns(copy, raw, width, tag=None):
            grouped = staging(width, tag)
            copy(
                out=grouped[:].rearrange("p (u v i) -> p u i v", v=PACK, i=PACK),
                in_=raw.rearrange("p i (u v) -> p u i v", v=PACK),
            )
            return grouped

        picked0 = [ring.tile([P, PACK, HALF], F32, name=f"picked0{h}", tag="wide") for h in range(2)]
        picked1 = {}

        def gather(r, dst, j0, width):
            h, o = divmod(j0, HALF)
            nc.vector.tensor_tensor(
                dst, x_sb[r][:].indirect(offsets[:, j0 // LIST_ROWS:(j0 + width) // LIST_ROWS]),
                wgt_sb[h][:, o:o + width], ALU.mult,
            )

        def gather0(r, h):
            gather(r, picked0[h][:, r, :], h * HALF, HALF)

        def gather1(r, q, tag="picked1", bufs=3):
            if q not in picked1:
                picked1.setdefault(q, ring.tile([P, PACK, CHUNKS[q]], F32, name="picked1", tag=tag, bufs=bufs, align_bytes=64))
            gather(r, picked1[q][:, r - PACK, :], STARTS[q], CHUNKS[q])

        wq_mx = [mx_tiles(f"wq{a}", N) for a in range(2)]
        wr_mx = [mx_tiles(f"wr{a}", N) for a in range(2)]
        wx_mx = mx_tiles("wx", N)
        xg0_mx = [mx_tiles(f"xg0{h}", HALF) for h in range(2)]
        xg1_mx = [mx_tiles(f"xg1{q}", w) for q, w in enumerate(CHUNKS)]
        c_mx = [mx_tiles(f"cq{h}", HALF) for h in range(2)]
        y_mx = mx_tiles("y", J)

        def bank(n):
            return psum.tile([P, 512], F32, name=f"bank{n}", tag=f"bank{n}")

        def first_tier(a, copy, tag=None):
            quantize(wq_mx[a], slice(0, N), round_weights(copy, wt_sb[a], tag)[:])

        def second_tier(a, tag=None):
            grouped = staging(N, tag)
            dealt = grouped[:].rearrange("p (t m i) -> p t m i", t=PACK, i=PACK)
            raw = wt_sb[a][:].rearrange("p i (m t) -> p i m t", t=PACK)
            for s in range(4):
                t0, m0 = 2 * (s // 2), MH * (s % 2)
                back = bank(4 + s)[:].rearrange("p (i t m) -> p i t m", i=PACK, t=2)
                for i in range(PACK):
                    for t in range(2):
                        col = (t0 + t) * P + m0
                        matmul(back[:, i, t, :], eye_mx, slice(i * P, (i + 1) * P), wq_mx[a], slice(col, col + MH), True, True)
                nc.vector.tensor_tensor(
                    dealt[:, t0:t0 + 2, m0:m0 + MH, :].rearrange("p t m i -> p m i t"),
                    raw[:, :, m0:m0 + MH, t0:t0 + 2].rearrange("p i m t -> p m i t"),
                    back.rearrange("p i t m -> p m i t"),
                    ALU.subtract,
                )
            quantize(wr_mx[a], slice(0, N), grouped[:])

        out_rows = out_0.rearrange("(p t) j -> p t j", t=PACK)
        words = out_1[0].rearrange("p j i -> p (j i)").bitcast(I32)
        results = {}

        def front(q, tag=None, copy=nc.scalar.copy):
            quantize(xg1_mx[q], slice(0, CHUNKS[q]), round_columns(copy, picked1[q][:], CHUNKS[q], tag)[:])

        def features(quarter, copy, tag=None):
            h, o = divmod(quarter * CHUNK, HALF)
            quantize(c_mx[h], slice(o, o + CHUNK), round_columns(copy, c_sb[h][:, :, o:o + CHUNK], CHUNK, tag)[:])

        def product(q, on_vector):
            width = CHUNKS[q]
            h, o = divmod(STARTS[q], HALF)
            half_cols = slice(o, o + width)
            own_cols = slice(0, width)
            per_bank = 512 // width
            y = keep.tile([P, PACK, width], F32, name=f"y{q}")
            results.setdefault(q, y)
            terms = [(wq_mx[0], xg0_mx[h], half_cols), (wr_mx[0], xg0_mx[h], half_cols), (wx_mx, c_mx[h], half_cols),
                     (wq_mx[1], xg1_mx[q], own_cols), (wr_mx[1], xg1_mx[q], own_cols)]
            for t0 in range(0, PACK, per_bank):
                acc = bank((STARTS[q] * PACK + t0 * width) // 512)[:].rearrange("p (t j) -> p t j", t=per_bank)
                for n, (lhs, rhs, cols) in enumerate(terms):
                    for t in range(per_bank):
                        w_cols = slice((t0 + t) * P, (t0 + t + 1) * P)
                        matmul(acc[:, t, :], lhs, w_cols, rhs, cols, n == 0 and t == 0,
                               n == len(terms) - 1 and t == per_bank - 1)
                if t0 // per_bank in on_vector:
                    bias = b_sb[:, t0:t0 + per_bank].unsqueeze(2).to_broadcast([P, per_bank, width])
                    nc.vector.tensor_tensor(y[:, t0:t0 + per_bank, :], acc, bias, ALU.add)
                else:
                    for t in range(per_bank):
                        row = t0 + t
                        nc.scalar.activation(out=y[:, row, :], in_=acc[:, t, :], func=ACT.Identity, bias=b_sb[:, row:row + 1])
                nc.sync.dma_start(out=out_rows[:, t0:t0 + per_bank, STARTS[q]:STARTS[q] + width], in_=y[:, t0:t0 + per_bank, :])

        def planes(q, copy, tag=None):
            j_cols = slice(STARTS[q], STARTS[q] + CHUNKS[q])
            quantize(y_mx, j_cols, round_columns(copy, results[q][:], CHUNKS[q], tag)[:])
            if q in CODE_STORES:
                done = slice(CODE_STORES[q], STARTS[q] + CHUNKS[q])
                nc.sync.dma_start(out=words[:, done], in_=y_mx[0][:, done].bitcast(I32))

        quantize(wq_mx[0], slice(0, N), round_weights_shared(wt_sb[0])[:])
        gather0(0, 0)
        gather0(0, 1)
        second_tier(0, "held0")
        first_tier(1, scalar_copy)
        gather0(1, 0)
        gather0(1, 1)
        gather0(2, 0)
        gather0(2, 1)
        quantize(wx_mx, slice(0, N), round_weights(scalar_copy, wx_sb)[:])
        gather0(3, 0)
        gather0(3, 1)
        second_tier(1, "held3")
        quantize(xg0_mx[0], slice(0, HALF), round_columns(nc.scalar.copy, picked0[0][:], HALF)[:])
        quantize(xg0_mx[1], slice(0, HALF), round_columns(nc.scalar.copy, picked0[1][:], HALF)[:])
        gather1(4, 0)
        gather1(4, 1)
        gather1(4, 2)
        quantize(c_mx[0], slice(0, HALF), round_columns(nc.scalar.copy, c_sb[0][:], HALF)[:])
        gather1(5, 0)
        gather1(5, 1)
        gather1(5, 2)
        quantize(c_mx[1], slice(0, HALF), round_columns(nc.scalar.copy, c_sb[1][:], HALF)[:])
        gather1(6, 0)
        gather1(6, 1)
        gather1(6, 2)
        gather1(7, 0)
        gather1(7, 1)
        gather1(7, 2)
        front(0)
        front(1)
        product(0, ())
        gather1(4, 3)
        gather1(5, 3)
        gather1(6, 3)
        gather1(7, 3)
        front(2)
        product(1, (0, 1))
        front(3)
        gather1(4, 4)
        gather1(5, 4)
        gather1(6, 4)
        gather1(7, 4)
        front(4)
        product(2, (0, 1))
        product(3, (0,))
        product(4, (0,))
        planes(0, nc.scalar.copy)
        planes(1, nc.scalar.copy)
        planes(2, nc.scalar.copy)
        planes(3, nc.scalar.copy)
        planes(4, nc.vector.tensor_copy)

        scale_rows = out_2[0].bitcast(I32)
        for g in range(4):
            queue = nc.sync if g % 2 == 0 else nc.scalar
            queue.dma_start(out=scale_rows[4 * g:4 * g + 4, :], in_=y_mx[1][32 * g:32 * g + 4, :].bitcast(I32))
